import numpy as np
import ml_dtypes


def mxq(x, axis, fmt="e4m3"):
    dtype, down = {"e4m3": (ml_dtypes.float8_e4m3fn, 7), "e5m2": (ml_dtypes.float8_e5m2, 14)}[fmt]
    v = np.moveaxis(np.asarray(x, np.float32).astype(ml_dtypes.bfloat16).astype(np.float64), axis, -1)
    blocks = v.reshape(v.shape[:-1] + (-1, 32))
    amax = np.abs(blocks).max(-1, keepdims=True)
    byte = np.maximum(np.where(amax > 0, np.frexp(amax)[1] - 1 + 127, 0) - down, 1)
    scale = np.exp2(byte - 127.0)
    codes = (blocks / scale).astype(np.float32).astype(dtype).astype(np.float64)
    return np.moveaxis((codes * scale).reshape(v.shape), -1, axis)


WIDE = False


def mx_kscale(k):
    if not WIDE:
        return np.ones(k)
    levels = np.array([10, -10, 5, -5, 0])
    if k % 512:
        return np.exp2(np.random.permutation(np.resize(levels, k // 32))).repeat(32)
    a = np.empty((k // 512, 16))
    for p in range(k // 512):
        a[p, :8] = np.random.permutation(np.resize(levels, 8))
        for g in range(8):
            far = levels[np.abs(levels - a[p, g]) >= 10]
            a[p, g + 8] = far[np.random.randint(len(far))]
    return np.exp2(a.ravel()).repeat(32)


def f64(x):
    return np.asarray(x).astype(np.float64)


def striped(idx):
    return np.tile(np.asarray(idx).reshape(-1, 16).T, (8, 1)).astype(np.uint16)


def unstriped(offs):
    return offs[:16].T.reshape(-1).astype(np.int64)


E2M1 = np.array([0.0, 0.5, 1.0, 1.5, 2.0, 3.0, 4.0, 6.0, -0.0, -0.5, -1.0, -1.5, -2.0, -3.0, -4.0, -6.0])


def pack_weight(w, fmt):
    k, n = w.shape
    w = f64(np.asarray(w, np.float32).astype(ml_dtypes.bfloat16)).reshape(k // 32, 32, n)
    amax = np.abs(w).max(1)
    if fmt == "e4m3":
        byte = np.frexp(amax)[1] - 1 + 127 - 7
    else:
        mant, ex = np.frexp(amax / 6.0)
        byte = np.where(mant > 0.5, ex, ex - 1) + 127
    byte = np.clip(np.where(amax > 0, byte, 1), 1, 254)
    scaled = (w * np.exp2(127.0 - byte)[:, None, :]).reshape(k, n).astype(np.float32)
    by_word = np.ascontiguousarray(scaled.reshape(k // 512, 128, 4, n).transpose(0, 1, 3, 2))
    if fmt == "e4m3":
        words = by_word.astype(ml_dtypes.float8_e4m3fn).view(np.uint8)
    else:
        c = by_word.astype(ml_dtypes.float4_e2m1fn).view(np.uint8) & 0xF
        words = (c[..., 0::2] | (c[..., 1::2] << 4)).reshape(k // 512, 128, 2 * n)
    return np.ascontiguousarray(words), np.ascontiguousarray(byte.astype(np.uint8).reshape(k // 512, 16, n))


def unpack_weight(words, scales, fmt):
    g, _, n = scales.shape
    words = np.ascontiguousarray(words).reshape(g, 128, n, -1)
    if fmt == "e4m3":
        vals = words.view(ml_dtypes.float8_e4m3fn).astype(np.float64)
    else:
        nib = np.empty((g, 128, n, 4), np.uint8)
        nib[..., 0::2] = words & 0xF
        nib[..., 1::2] = words >> 4
        vals = E2M1[nib]
    vals = vals * np.repeat(np.exp2(scales.astype(np.float64) - 127.0), 8, axis=1)[..., None]
    return vals.transpose(0, 1, 3, 2).reshape(g * 512, n)


D, T, I, J, U, E = 512, 2048, 512, 512, 1024, 512


def setup_inputs():
    n = np.random.standard_normal
    idx = np.random.permutation(T)[:I]
    idx2 = np.random.permutation(U)[:J]
    idx3 = np.random.permutation(U)[:J]
    idx4 = np.random.permutation(U)[:J]
    fd = mx_kscale(D)
    fi = mx_kscale(I)
    ti = np.ones(T)
    ti[idx] = fi
    keysp = pack_weight(n((D, T)) / fd[:, None], "e4m3")
    return {
        "keys_words": keysp[0],
        "keys_scales": keysp[1],
        "notes": (n((D, U)) * 1.0 / np.sqrt(D) * fd[:, None]).astype(np.float32),
        "rowf": (np.random.uniform(0.02, 0.08, (I, 1)) * fi[:, None]).astype(np.float32),
        "vals": (n((E, T)) / ti).astype(np.float32),
        "mem": (np.random.uniform(0.3, 1.0, (1, J))).astype(np.float32),
        "offs": striped(idx),
        "offs2": striped(idx2),
        "offs3": striped(idx3),
        "offs4": striped(idx4),
    }


def reference(keys_words, keys_scales, notes, rowf, vals, mem, offs, offs2, offs3, offs4):
    idx = unstriped(offs)
    idx2 = unstriped(offs2)
    idx3 = unstriped(offs3)
    idx4 = unstriped(offs4)
    keysu = unpack_weight(keys_words, keys_scales, "e4m3")
    keysidxg = keysu[:, idx]
    notesq = mxq(f64(notes), 0, "e4m3")
    g1 = keysidxg.T @ notesq
    lo2 = np.minimum(g1[:, idx2], g1[:, idx3])
    hi2 = np.maximum(g1[:, idx2], g1[:, idx3])
    g0 = np.maximum(lo2, np.minimum(hi2, g1[:, idx4]))
    gr1 = g0 * f64(rowf)
    vt1 = f64(vals)[:, idx].T
    vt1q = mxq(vt1, 0, "e4m3")
    gr1q = mxq(gr1, 0, "e4m3")
    o = vt1q.T @ gr1q
    o1 = np.pad(o, ((0, 0), (1, 0)))[:, :J]
    y = o - o1 * f64(mem)
    return y

@@ -1,0 +1,208 @@
+from contextlib import ExitStack
+
+import concourse.mybir as mybir
+from concourse.masks import make_identity
+
+D, T, I, J, U, E = 512, 2048, 512, 512, 1024, 512
+FLOPS = 2 * D * I * U + 2 * I * E * J
+
+F32 = mybir.dt.float32
+BF16 = mybir.dt.bfloat16
+I32 = mybir.dt.int32
+U32 = mybir.dt.uint32
+U16 = mybir.dt.uint16
+U8 = mybir.dt.uint8
+FP8X4 = mybir.dt.float8_e4m3fn_x4
+ALU = mybir.AluOpType
+COPY = mybir.ActivationFunctionType.Copy
+
+P = 128
+PACK = 4
+BANK = 512
+NOTE_PIECES = ((0, 512, 320), (512, 256, 256), (768, 256, 256))
+
+
+def tile_attend_tab_middleof3_changes_kernel(
+    tc, keys_words, keys_scales, notes, rowf, vals, mem, offs, offs2, offs3, offs4, out
+):
+    nc = tc.nc
+    with ExitStack() as ctx:
+        held = ctx.enter_context(tc.tile_pool(name="held", bufs=1))
+        work = ctx.enter_context(tc.tile_pool(name="work", bufs=4))
+        acc_pool = ctx.enter_context(tc.psum_pool(name="acc", bufs=6))
+        turn_pool = ctx.enter_context(tc.psum_pool(name="turn", bufs=2))
+
+        token_list = held.tile([P, I // 16], U16, name="token_list")
+        nc.sync.dma_start(token_list[:], offs)
+        key_words = held.tile([P, T], I32, name="key_words")
+        nc.sync.dma_start(key_words[:], keys_words[0].rearrange("p n t -> p (n t)").bitcast(I32))
+
+        key_scales = held.tile([P, T], U8, name="key_scales")
+        nc.vector.memset(key_scales[:].bitcast(I32), 0)
+        for q in range(4):
+            nc.sync.dma_start(
+                key_scales[32 * q : 32 * q + 4, :].bitcast(I32),
+                keys_scales[0, 4 * q : 4 * q + 4, :].bitcast(I32),
+            )
+
+        row_factor = held.tile([P, PACK], F32, name="row_factor")
+        nc.sync.dma_start(row_factor[:], rowf.rearrange("(p t) o -> p (t o)", t=PACK))
+
+        notes_raw = []
+        for n, (u0, width, share) in enumerate(NOTE_PIECES):
+            raw = held.tile([P, PACK, width], F32, name=f"notes_raw{n}")
+            nc.sync.dma_start(raw[:], notes[:, u0 : u0 + width].rearrange("(p t) u -> p t u", t=PACK))
+            notes_raw.append(raw)
+
+        column_lists = []
+        for n, source in enumerate((offs2, offs3, offs4)):
+            column_list = held.tile([P, J // 16], U16, name=f"column_list{n}")
+            nc.sync.dma_start(column_list[:], source)
+            column_lists.append(column_list)
+
+        vals_pool = []
+        for m in range(E // P):
+            pool_rows = held.tile([P, T], F32, name=f"vals_pool{m}")
+            nc.sync.dma_start(pool_rows[:], vals[m * P : (m + 1) * P, :])
+            vals_pool.append(pool_rows)
+
+        memory = held.tile([P, J], F32, name="memory")
+        nc.sync.dma_start(memory[:], mem[0].partition_broadcast(P))
+
+        identity = held.tile([P, P], F32, name="identity")
+        make_identity(nc, identity[:])
+
+        carried = held.tile([P, E // P, J], F32, name="carried")
+        nc.vector.memset(carried[:, :, 0:1], 0.0)
+
+        factor_rows = held.tile([P, PACK, J], F32, name="factor_rows")
+        nc.scalar.copy(factor_rows[:], row_factor[:].unsqueeze(2).to_broadcast([P, PACK, J]))
+
+        picked_scales = held.tile([P, I], U8, name="picked_scales", align_bytes=64)
+        nc.vector.tensor_copy(
+            picked_scales[:].rearrange("p (t s) -> p s t", t=PACK),
+            key_scales[:].indirect(token_list[:]),
+        )
+        picked_words = held.tile([P, I], U32, name="picked_words", align_bytes=64)
+        nc.vector.tensor_copy(
+            picked_words[:].rearrange("p (t s) -> p s t", t=PACK),
+            key_words[:].bitcast(U32).indirect(token_list[:]),
+        )
+
+        note_codes, note_scales = [], []
+        for n, (u0, width, share) in enumerate(NOTE_PIECES):
+            grouped = held.tile([P, width, PACK], BF16, name=f"notes_grouped{n}", align_bytes=64)
+            nc.vector.tensor_copy(
+                grouped[:, :share, :].rearrange("p (c i) t -> p c t i", i=4),
+                notes_raw[n][:, :, :share].rearrange("p t (c i) -> p c t i", i=4),
+            )
+            if share < width:
+                nc.scalar.copy(
+                    grouped[:, share:, :].rearrange("p (c i) t -> p c t i", i=4),
+                    notes_raw[n][:, :, share:].rearrange("p t (c i) -> p c t i", i=4),
+                )
+            codes = held.tile([P, width], U32, name=f"note_codes{n}", align_bytes=64)
+            scales = held.tile([P, width], U8, name=f"note_scales{n}", align_bytes=64)
+            nc.vector.quantize_mx(
+                out=codes[:].bitcast(FP8X4), scales=scales[:], in_=grouped[:].rearrange("p u t -> p (u t)")
+            )
+            note_codes.append(codes)
+            note_scales.append(scales)
+
+        table = [work.tile([P, U], F32, name="table") for t in range(PACK)]
+        banks = {}
+        for half in range(U // BANK):
+            for t in range(PACK):
+                banks[half, t] = acc_pool.tile([P, BANK], F32, name="acc")
+            for n, (u0, width, share) in enumerate(NOTE_PIECES):
+                if u0 // BANK != half:
+                    continue
+                for t in range(PACK):
+                    nc.tensor.matmul_mx(
+                        out=banks[half, t][:, u0 % BANK : u0 % BANK + width],
+                        lhsT=picked_words[:, t * P : (t + 1) * P].bitcast(FP8X4),
+                        lhsT_scale=picked_scales[:, t * P : (t + 1) * P],
+                        rhs=note_codes[n][:].bitcast(FP8X4),
+                        rhs_scale=note_scales[n][:],
+                        start=True,
+                        stop=True,
+                    )
+            if half == 0:
+                for t in range(PACK):
+                    nc.scalar.copy(table[t][:, :BANK], banks[0, t][:])
+
+        lower = held.tile([P, PACK, J], F32, name="lower")
+        capped = held.tile([P, PACK, J], F32, name="capped")
+        nc.vector.tensor_copy(table[0][:, BANK:], banks[1, 0][:])
+        for t in range(PACK):
+            if t + 1 < PACK:
+                nc.scalar.copy(table[t + 1][:, BANK:], banks[1, t + 1][:])
+            first = work.tile([P, J], F32, name="first")
+            second = work.tile([P, J], F32, name="second")
+            third = work.tile([P, J], F32, name="third")
+            upper = work.tile([P, J], F32, name="upper")
+            nc.scalar.activation(first[:], table[t][:].indirect(column_lists[0][:]), COPY)
+            nc.vector.tensor_tensor(second[:], table[t][:].indirect(column_lists[1][:]), factor_rows[:, t, :], ALU.mult)
+            nc.scalar.activation(third[:], table[t][:].indirect(column_lists[2][:]), COPY)
+            factor = row_factor[:, t : t + 1]
+            nc.vector.scalar_tensor_tensor(upper[:], first[:], factor, second[:], ALU.mult, ALU.max)
+            nc.vector.scalar_tensor_tensor(lower[:, t, :], first[:], factor, second[:], ALU.mult, ALU.min)
+            nc.vector.scalar_tensor_tensor(capped[:, t, :], third[:], factor, upper[:], ALU.mult, ALU.min)
+
+        middle = held.tile([P, J, PACK], BF16, name="middle", align_bytes=64)
+        nc.vector.tensor_tensor(
+            middle[:].rearrange("p (c i) t -> p c t i", i=4),
+            lower[:].rearrange("p t (c i) -> p c t i", i=4),
+            capped[:].rearrange("p t (c i) -> p c t i", i=4),
+            ALU.max,
+        )
+        middle_codes = held.tile([P, J], U32, name="middle_codes", align_bytes=64)
+        middle_scales = held.tile([P, J], U8, name="middle_scales", align_bytes=64)
+        nc.vector.quantize_mx(
+            out=middle_codes[:].bitcast(FP8X4), scales=middle_scales[:], in_=middle[:].rearrange("p j t -> p (j t)")
+        )
+
+        def value_product(m):
+            picked_vals = work.tile([P, I], BF16, name="table")
+            nc.scalar.activation(picked_vals[:], vals_pool[m][:].indirect(token_list[:]), COPY)
+            pairs = picked_vals[:].bitcast(F32)
+            turned = turn_pool.tile([P, 2, P], F32, name="turned")
+            for u in range(2):
+                nc.tensor.transpose(turned[:, u, :], pairs[:, u : I // 2 : 2], identity[:])
+            val_pairs = held.tile([P, P, 2], F32, name=f"val_pairs{m}", align_bytes=64)
+            nc.scalar.copy(val_pairs[:], turned[:].rearrange("p u e -> p e u"))
+            val_codes = held.tile([P, P], U32, name=f"val_codes{m}", align_bytes=64)
+            val_scales = held.tile([P, P], U8, name=f"val_scales{m}", align_bytes=64)
+            nc.vector.quantize_mx(
+                out=val_codes[:].bitcast(FP8X4),
+                scales=val_scales[:],
+                in_=val_pairs[:].rearrange("p e u -> p (e u)").bitcast(BF16),
+            )
+            total = acc_pool.tile([P, J], F32, name="acc")
+            nc.tensor.matmul_mx(
+                out=total[:],
+                lhsT=val_codes[:].bitcast(FP8X4),
+                lhsT_scale=val_scales[:],
+                rhs=middle_codes[:].bitcast(FP8X4),
+                rhs_scale=middle_scales[:],
+                start=True,
+                stop=True,
+            )
+            return total
+
+        def carry(m):
+            nc.vector.tensor_tensor(carried[:, m, 1:], sums[m][:, : J - 1], memory[:, 1:], ALU.mult)
+
+        def finish(m):
+            result = held.tile([P, J], F32, name=f"result{m}")
+            nc.vector.tensor_tensor(result[:], sums[m][:], carried[:, m, :], ALU.subtract)
+            nc.sync.dma_start(out[m * P : (m + 1) * P, :], result[:])
+
+        sums = [value_product(0)]
+        for m in range(E // P):
+            if m + 1 < E // P:
+                sums.append(value_product(m + 1))
+            carry(m)
+            if m > 0:
+                finish(m - 1)
+        finish(E // P - 1)

@@ -19,7 +19,7 @@ COPY = mybir.ActivationFunctionType.Copy
 P = 128
 PACK = 4
 BANK = 512
-NOTE_PIECES = ((0, 512, 320), (512, 256, 256), (768, 256, 256))
+NOTE_PIECES = ((0, 256, 0), (256, 256, 0), (512, 256, 256), (768, 256, 256))
 
 
 def tile_attend_tab_middleof3_changes_kernel(
@@ -34,6 +34,8 @@ def tile_attend_tab_middleof3_changes_kernel(
 
         token_list = held.tile([P, I // 16], U16, name="token_list")
         nc.sync.dma_start(token_list[:], offs)
+        row_factor = held.tile([P, PACK], F32, name="row_factor")
+        nc.sync.dma_start(row_factor[:], rowf.rearrange("(p t) o -> p (t o)", t=PACK))
         key_words = held.tile([P, T], I32, name="key_words")
         nc.sync.dma_start(key_words[:], keys_words[0].rearrange("p n t -> p (n t)").bitcast(I32))
 
@@ -44,9 +46,6 @@ def tile_attend_tab_middleof3_changes_kernel(
                 key_scales[32 * q : 32 * q + 4, :].bitcast(I32),
                 keys_scales[0, 4 * q : 4 * q + 4, :].bitcast(I32),
             )
-
-        row_factor = held.tile([P, PACK], F32, name="row_factor")
-        nc.sync.dma_start(row_factor[:], rowf.rearrange("(p t) o -> p (t o)", t=PACK))
 
         notes_raw = []
         for n, (u0, width, share) in enumerate(NOTE_PIECES):
@@ -72,8 +71,11 @@ def tile_attend_tab_middleof3_changes_kernel(
         identity = held.tile([P, P], F32, name="identity")
         make_identity(nc, identity[:])
 
-        carried = held.tile([P, E // P, J], F32, name="carried")
-        nc.vector.memset(carried[:, :, 0:1], 0.0)
+        carried = []
+        for m in range(E // P):
+            shifted = held.tile([P, J], F32, name=f"carried{m}", align_bytes=64)
+            nc.vector.memset(shifted[:, 0:1], 0.0)
+            carried.append(shifted)
 
         factor_rows = held.tile([P, PACK, J], F32, name="factor_rows")
         nc.scalar.copy(factor_rows[:], row_factor[:].unsqueeze(2).to_broadcast([P, PACK, J]))
@@ -92,7 +94,8 @@ def tile_attend_tab_middleof3_changes_kernel(
         note_codes, note_scales = [], []
         for n, (u0, width, share) in enumerate(NOTE_PIECES):
             grouped = held.tile([P, width, PACK], BF16, name=f"notes_grouped{n}", align_bytes=64)
-            nc.vector.tensor_copy(
+            if share > 0:
+              nc.vector.tensor_copy(
                 grouped[:, :share, :].rearrange("p (c i) t -> p c t i", i=4),
                 notes_raw[n][:, :, :share].rearrange("p t (c i) -> p c t i", i=4),
             )
@@ -109,7 +112,7 @@ def tile_attend_tab_middleof3_changes_kernel(
             note_codes.append(codes)
             note_scales.append(scales)
 
-        table = [work.tile([P, U], F32, name="table") for t in range(PACK)]
+        table = [held.tile([P, U], F32, name=f"table{t}") for t in range(PACK)]
         banks = {}
         for half in range(U // BANK):
             for t in range(PACK):
@@ -162,8 +165,8 @@ def tile_attend_tab_middleof3_changes_kernel(
             out=middle_codes[:].bitcast(FP8X4), scales=middle_scales[:], in_=middle[:].rearrange("p j t -> p (j t)")
         )
 
-        def value_product(m):
-            picked_vals = work.tile([P, I], BF16, name="table")
+        def value_product(m, val_codes):
+            picked_vals = held.tile([P, I], BF16, name=f"table{2 + min(m, 1)}")
             nc.scalar.activation(picked_vals[:], vals_pool[m][:].indirect(token_list[:]), COPY)
             pairs = picked_vals[:].bitcast(F32)
             turned = turn_pool.tile([P, 2, P], F32, name="turned")
@@ -171,17 +174,16 @@ def tile_attend_tab_middleof3_changes_kernel(
                 nc.tensor.transpose(turned[:, u, :], pairs[:, u : I // 2 : 2], identity[:])
             val_pairs = held.tile([P, P, 2], F32, name=f"val_pairs{m}", align_bytes=64)
             nc.scalar.copy(val_pairs[:], turned[:].rearrange("p u e -> p e u"))
-            val_codes = held.tile([P, P], U32, name=f"val_codes{m}", align_bytes=64)
             val_scales = held.tile([P, P], U8, name=f"val_scales{m}", align_bytes=64)
             nc.vector.quantize_mx(
-                out=val_codes[:].bitcast(FP8X4),
+                out=val_codes.bitcast(FP8X4),
                 scales=val_scales[:],
                 in_=val_pairs[:].rearrange("p e u -> p (e u)").bitcast(BF16),
             )
             total = acc_pool.tile([P, J], F32, name="acc")
             nc.tensor.matmul_mx(
                 out=total[:],
-                lhsT=val_codes[:].bitcast(FP8X4),
+                lhsT=val_codes.bitcast(FP8X4),
                 lhsT_scale=val_scales[:],
                 rhs=middle_codes[:].bitcast(FP8X4),
                 rhs_scale=middle_scales[:],
@@ -191,18 +193,21 @@ def tile_attend_tab_middleof3_changes_kernel(
             return total
 
         def carry(m):
-            nc.vector.tensor_tensor(carried[:, m, 1:], sums[m][:, : J - 1], memory[:, 1:], ALU.mult)
+            nc.vector.tensor_tensor(carried[m][:, 1:], sums[m][:, : J - 1], memory[:, 1:], ALU.mult)
 
         def finish(m):
             result = held.tile([P, J], F32, name=f"result{m}")
-            nc.vector.tensor_tensor(result[:], sums[m][:], carried[:, m, :], ALU.subtract)
+            nc.vector.tensor_tensor(result[:], sums[m][:], carried[m][:], ALU.subtract)
             nc.sync.dma_start(out[m * P : (m + 1) * P, :], result[:])
 
-        sums = [value_product(0)]
-        for m in range(E // P):
-            if m + 1 < E // P:
-                sums.append(value_product(m + 1))
+        early_codes = held.tile([P, 2 * P], U32, name="middle", align_bytes=64)
+        sums = [value_product(m, early_codes[:, m * P : (m + 1) * P]) for m in range(2)]
+        carry(0)
+        carry(1)
+        for m in range(2):
+            finish(m)
+            late_codes = held.tile([P, P], U32, name=f"carried{m}", align_bytes=64)
+            sums.append(value_product(2 + m, late_codes[:]))
+        for m in range(2, 4):
             carry(m)
-            if m > 0:
-                finish(m - 1)
-        finish(E // P - 1)
+            finish(m)

@@ -19,7 +19,20 @@ COPY = mybir.ActivationFunctionType.Copy
 P = 128
 PACK = 4
 BANK = 512
-NOTE_PIECES = ((0, 256, 0), (256, 256, 0), (512, 256, 256), (768, 256, 256))
+LIST_GROUP = 16
+QUADRANT = 32
+LINE = 4
+PIECE = 256
+SHARED_PIECE = 1
+HALF = J // 2
+VALUE_TILES = E // P
+
+
+def by_lines(interleaved, planes):
+    return (
+        interleaved.rearrange("p (c i) t -> p c t i", i=LINE),
+        [plane.rearrange("p t (c i) -> p c t i", i=LINE) for plane in planes],
+    )
 
 
 def tile_attend_tab_middleof3_changes_kernel(
@@ -28,39 +41,43 @@ def tile_attend_tab_middleof3_changes_kernel(
     nc = tc.nc
     with ExitStack() as ctx:
         held = ctx.enter_context(tc.tile_pool(name="held", bufs=1))
-        work = ctx.enter_context(tc.tile_pool(name="work", bufs=4))
-        acc_pool = ctx.enter_context(tc.psum_pool(name="acc", bufs=6))
-        turn_pool = ctx.enter_context(tc.psum_pool(name="turn", bufs=2))
+        work = ctx.enter_context(tc.tile_pool(name="work", bufs=PACK))
+        shared = ctx.enter_context(tc.tile_pool(name="shared", bufs=1))
+        psum = ctx.enter_context(tc.psum_pool(name="psum", bufs=1))
 
-        token_list = held.tile([P, I // 16], U16, name="token_list")
-        nc.sync.dma_start(token_list[:], offs)
+        def load_list(name, source):
+            entries = held.tile([P, J // LIST_GROUP], U16, name=name)
+            nc.sync.dma_start(entries[:], source)
+            return entries
+
+        def load_notes(n):
+            raw = held.tile([P, PACK, PIECE], F32, name=f"notes_raw{n}")
+            columns = notes[:, n * PIECE : (n + 1) * PIECE]
+            nc.sync.dma_start(raw[:], columns.rearrange("(p t) u -> p t u", t=PACK))
+            return raw
+
+        token_list = load_list("token_list", offs)
         row_factor = held.tile([P, PACK], F32, name="row_factor")
         nc.sync.dma_start(row_factor[:], rowf.rearrange("(p t) o -> p (t o)", t=PACK))
-        key_words = held.tile([P, T], I32, name="key_words")
-        nc.sync.dma_start(key_words[:], keys_words[0].rearrange("p n t -> p (n t)").bitcast(I32))
+        notes_raw = [load_notes(0)]
 
         key_scales = held.tile([P, T], U8, name="key_scales")
         nc.vector.memset(key_scales[:].bitcast(I32), 0)
-        for q in range(4):
+        for q in range(P // QUADRANT):
             nc.sync.dma_start(
-                key_scales[32 * q : 32 * q + 4, :].bitcast(I32),
+                key_scales[QUADRANT * q : QUADRANT * q + 4, :].bitcast(I32),
                 keys_scales[0, 4 * q : 4 * q + 4, :].bitcast(I32),
             )
+        key_words = held.tile([P, T], I32, name="key_words")
+        nc.sync.dma_start(key_words[:], keys_words[0].rearrange("p n t -> p (n t)").bitcast(I32))
+        notes_raw.extend(load_notes(n) for n in range(1, U // PIECE))
 
-        notes_raw = []
-        for n, (u0, width, share) in enumerate(NOTE_PIECES):
-            raw = held.tile([P, PACK, width], F32, name=f"notes_raw{n}")
-            nc.sync.dma_start(raw[:], notes[:, u0 : u0 + width].rearrange("(p t) u -> p t u", t=PACK))
-            notes_raw.append(raw)
-
-        column_lists = []
-        for n, source in enumerate((offs2, offs3, offs4)):
-            column_list = held.tile([P, J // 16], U16, name=f"column_list{n}")
-            nc.sync.dma_start(column_list[:], source)
-            column_lists.append(column_list)
+        first_list = load_list("first_list", offs2)
+        second_list = load_list("second_list", offs3)
+        third_list = load_list("third_list", offs4)
 
         vals_pool = []
-        for m in range(E // P):
+        for m in range(VALUE_TILES):
             pool_rows = held.tile([P, T], F32, name=f"vals_pool{m}")
             nc.sync.dma_start(pool_rows[:], vals[m * P : (m + 1) * P, :])
             vals_pool.append(pool_rows)
@@ -72,7 +89,7 @@ def tile_attend_tab_middleof3_changes_kernel(
         make_identity(nc, identity[:])
 
         carried = []
-        for m in range(E // P):
+        for m in range(VALUE_TILES):
             shifted = held.tile([P, J], F32, name=f"carried{m}", align_bytes=64)
             nc.vector.memset(shifted[:, 0:1], 0.0)
             carried.append(shifted)
@@ -91,123 +108,151 @@ def tile_attend_tab_middleof3_changes_kernel(
             key_words[:].bitcast(U32).indirect(token_list[:]),
         )
 
-        note_codes, note_scales = [], []
-        for n, (u0, width, share) in enumerate(NOTE_PIECES):
-            grouped = held.tile([P, width, PACK], BF16, name=f"notes_grouped{n}", align_bytes=64)
-            if share > 0:
-              nc.vector.tensor_copy(
-                grouped[:, :share, :].rearrange("p (c i) t -> p c t i", i=4),
-                notes_raw[n][:, :, :share].rearrange("p t (c i) -> p c t i", i=4),
-            )
-            if share < width:
-                nc.scalar.copy(
-                    grouped[:, share:, :].rearrange("p (c i) t -> p c t i", i=4),
-                    notes_raw[n][:, :, share:].rearrange("p t (c i) -> p c t i", i=4),
-                )
-            codes = held.tile([P, width], U32, name=f"note_codes{n}", align_bytes=64)
-            scales = held.tile([P, width], U8, name=f"note_scales{n}", align_bytes=64)
+        def round_notes(n):
+            grouped = held.tile([P, PIECE, PACK], BF16, name=f"notes_grouped{n}", align_bytes=64)
+            split = PIECE // 2 if n == SHARED_PIECE else PIECE
+            target, (source,) = by_lines(grouped[:, :split, :], [notes_raw[n][:, :, :split]])
+            nc.vector.tensor_copy(target, source)
+            if split < PIECE:
+                target, (source,) = by_lines(grouped[:, split:, :], [notes_raw[n][:, :, split:]])
+                nc.scalar.copy(target, source)
+            return grouped
+
+        def quantise_notes(n):
+            codes = held.tile([P, PIECE], U32, name=f"note_codes{n}", align_bytes=64)
+            scales = held.tile([P, PIECE], U8, name=f"note_scales{n}", align_bytes=64)
             nc.vector.quantize_mx(
-                out=codes[:].bitcast(FP8X4), scales=scales[:], in_=grouped[:].rearrange("p u t -> p (u t)")
+                out=codes[:].bitcast(FP8X4),
+                scales=scales[:],
+                in_=notes_grouped[n][:].rearrange("p u t -> p (u t)"),
             )
-            note_codes.append(codes)
-            note_scales.append(scales)
+            return codes, scales
+
+        notes_grouped = [round_notes(0)]
+        notes_mx = []
+        for n in range(U // PIECE):
+            if n + 1 < U // PIECE:
+                notes_grouped.append(round_notes(n + 1))
+            notes_mx.append(quantise_notes(n))
 
         table = [held.tile([P, U], F32, name=f"table{t}") for t in range(PACK)]
-        banks = {}
-        for half in range(U // BANK):
-            for t in range(PACK):
-                banks[half, t] = acc_pool.tile([P, BANK], F32, name="acc")
-            for n, (u0, width, share) in enumerate(NOTE_PIECES):
-                if u0 // BANK != half:
-                    continue
-                for t in range(PACK):
-                    nc.tensor.matmul_mx(
-                        out=banks[half, t][:, u0 % BANK : u0 % BANK + width],
-                        lhsT=picked_words[:, t * P : (t + 1) * P].bitcast(FP8X4),
-                        lhsT_scale=picked_scales[:, t * P : (t + 1) * P],
-                        rhs=note_codes[n][:].bitcast(FP8X4),
-                        rhs_scale=note_scales[n][:],
-                        start=True,
-                        stop=True,
-                    )
-            if half == 0:
-                for t in range(PACK):
-                    nc.scalar.copy(table[t][:, :BANK], banks[0, t][:])
+        banks = [psum.tile([P, BANK], F32, name=f"bank{b}") for b in range(2 * PACK)]
+        for b in range(2 * PACK):
+            half, t = divmod(b, PACK)
+            for column in range(0, BANK, PIECE):
+                codes, scales = notes_mx[(half * BANK + column) // PIECE]
+                nc.tensor.matmul_mx(
+                    out=banks[b][:, column : column + PIECE],
+                    lhsT=picked_words[:, t * P : (t + 1) * P].bitcast(FP8X4),
+                    lhsT_scale=picked_scales[:, t * P : (t + 1) * P],
+                    rhs=codes[:].bitcast(FP8X4),
+                    rhs_scale=scales[:],
+                    start=True,
+                    stop=True,
+                )
+        for t in range(PACK):
+            nc.scalar.copy(table[t][:, :BANK], banks[t][:])
 
         lower = held.tile([P, PACK, J], F32, name="lower")
         capped = held.tile([P, PACK, J], F32, name="capped")
-        nc.vector.tensor_copy(table[0][:, BANK:], banks[1, 0][:])
+
+        def look_up_second(t):
+            second = work.tile([P, J], F32, name="second")
+            nc.vector.tensor_tensor(second[:], table[t][:].indirect(second_list[:]), factor_rows[:, t, :], ALU.mult)
+            return second
+
+        nc.vector.tensor_copy(table[0][:, BANK:], banks[PACK][:])
+        seconds = [look_up_second(0)]
         for t in range(PACK):
             if t + 1 < PACK:
-                nc.scalar.copy(table[t + 1][:, BANK:], banks[1, t + 1][:])
+                nc.scalar.copy(table[t + 1][:, BANK:], banks[PACK + t + 1][:])
+                seconds.append(look_up_second(t + 1))
             first = work.tile([P, J], F32, name="first")
-            second = work.tile([P, J], F32, name="second")
             third = work.tile([P, J], F32, name="third")
             upper = work.tile([P, J], F32, name="upper")
-            nc.scalar.activation(first[:], table[t][:].indirect(column_lists[0][:]), COPY)
-            nc.vector.tensor_tensor(second[:], table[t][:].indirect(column_lists[1][:]), factor_rows[:, t, :], ALU.mult)
-            nc.scalar.activation(third[:], table[t][:].indirect(column_lists[2][:]), COPY)
+            nc.scalar.activation(first[:], table[t][:].indirect(first_list[:]), COPY)
+            nc.scalar.activation(third[:], table[t][:].indirect(third_list[:]), COPY)
             factor = row_factor[:, t : t + 1]
-            nc.vector.scalar_tensor_tensor(upper[:], first[:], factor, second[:], ALU.mult, ALU.max)
-            nc.vector.scalar_tensor_tensor(lower[:, t, :], first[:], factor, second[:], ALU.mult, ALU.min)
+            nc.vector.scalar_tensor_tensor(upper[:], first[:], factor, seconds[t][:], ALU.mult, ALU.max)
+            nc.vector.scalar_tensor_tensor(lower[:, t, :], first[:], factor, seconds[t][:], ALU.mult, ALU.min)
             nc.vector.scalar_tensor_tensor(capped[:, t, :], third[:], factor, upper[:], ALU.mult, ALU.min)
 
-        middle = held.tile([P, J, PACK], BF16, name="middle", align_bytes=64)
-        nc.vector.tensor_tensor(
-            middle[:].rearrange("p (c i) t -> p c t i", i=4),
-            lower[:].rearrange("p t (c i) -> p c t i", i=4),
-            capped[:].rearrange("p t (c i) -> p c t i", i=4),
-            ALU.max,
-        )
+        half_bytes = HALF * PACK * 2
+        middle = []
+        for h in range(2):
+            rounded = shared.tile([P, HALF, PACK], BF16, name=f"middle{h}", align_bytes=64, offset=h * half_bytes)
+            columns = slice(h * HALF, (h + 1) * HALF)
+            target, (low, cap) = by_lines(rounded[:], [lower[:, :, columns], capped[:, :, columns]])
+            nc.vector.tensor_tensor(target, low, cap, ALU.max)
+            middle.append(rounded)
         middle_codes = held.tile([P, J], U32, name="middle_codes", align_bytes=64)
         middle_scales = held.tile([P, J], U8, name="middle_scales", align_bytes=64)
-        nc.vector.quantize_mx(
-            out=middle_codes[:].bitcast(FP8X4), scales=middle_scales[:], in_=middle[:].rearrange("p j t -> p (j t)")
-        )
 
-        def value_product(m, val_codes):
-            picked_vals = held.tile([P, I], BF16, name=f"table{2 + min(m, 1)}")
+        def quantise_middle(h):
+            columns = slice(h * HALF, (h + 1) * HALF)
+            nc.vector.quantize_mx(
+                out=middle_codes[:, columns].bitcast(FP8X4),
+                scales=middle_scales[:, columns],
+                in_=middle[h][:].rearrange("p j t -> p (j t)"),
+            )
+
+        def quantise_values(m, picked_vals, val_codes):
             nc.scalar.activation(picked_vals[:], vals_pool[m][:].indirect(token_list[:]), COPY)
             pairs = picked_vals[:].bitcast(F32)
-            turned = turn_pool.tile([P, 2, P], F32, name="turned")
+            turned = psum.tile([P, 2, P], F32, name=f"bank{m}")
             for u in range(2):
                 nc.tensor.transpose(turned[:, u, :], pairs[:, u : I // 2 : 2], identity[:])
             val_pairs = held.tile([P, P, 2], F32, name=f"val_pairs{m}", align_bytes=64)
             nc.scalar.copy(val_pairs[:], turned[:].rearrange("p u e -> p e u"))
             val_scales = held.tile([P, P], U8, name=f"val_scales{m}", align_bytes=64)
             nc.vector.quantize_mx(
-                out=val_codes.bitcast(FP8X4),
+                out=val_codes[:].bitcast(FP8X4),
                 scales=val_scales[:],
                 in_=val_pairs[:].rearrange("p e u -> p (e u)").bitcast(BF16),
             )
-            total = acc_pool.tile([P, J], F32, name="acc")
+            return val_codes, val_scales
+
+        def multiply(m, columns):
+            val_codes, val_scales = values_mx[m]
             nc.tensor.matmul_mx(
-                out=total[:],
-                lhsT=val_codes.bitcast(FP8X4),
+                out=sums[m][:, columns],
+                lhsT=val_codes[:].bitcast(FP8X4),
                 lhsT_scale=val_scales[:],
-                rhs=middle_codes[:].bitcast(FP8X4),
-                rhs_scale=middle_scales[:],
+                rhs=middle_codes[:, columns].bitcast(FP8X4),
+                rhs_scale=middle_scales[:, columns],
                 start=True,
                 stop=True,
             )
-            return total
 
         def carry(m):
             nc.vector.tensor_tensor(carried[m][:, 1:], sums[m][:, : J - 1], memory[:, 1:], ALU.mult)
 
-        def finish(m):
+        def finish(m, width=J):
             result = held.tile([P, J], F32, name=f"result{m}")
-            nc.vector.tensor_tensor(result[:], sums[m][:], carried[m][:], ALU.subtract)
-            nc.sync.dma_start(out[m * P : (m + 1) * P, :], result[:])
+            for column in range(0, J, width):
+                columns = slice(column, column + width)
+                nc.vector.tensor_tensor(result[:, columns], sums[m][:, columns], carried[m][:, columns], ALU.subtract)
+                nc.sync.dma_start(out[m * P : (m + 1) * P, columns], result[:, columns])
 
-        early_codes = held.tile([P, 2 * P], U32, name="middle", align_bytes=64)
-        sums = [value_product(m, early_codes[:, m * P : (m + 1) * P]) for m in range(2)]
+        sums = [psum.tile([P, J], F32, name=f"bank{PACK + m}") for m in range(VALUE_TILES)]
+        values_mx = []
+        for m in range(2):
+            quantise_middle(m)
+            picked_vals = held.tile([P, I], BF16, name=f"table{2 + m}")
+            val_codes = shared.tile([P, P], U32, name=f"val_codes{m}", align_bytes=64, offset=m * half_bytes)
+            values_mx.append(quantise_values(m, picked_vals, val_codes))
+            multiply(0, slice(m * HALF, (m + 1) * HALF))
+        multiply(1, slice(0, J))
         carry(0)
         carry(1)
-        for m in range(2):
-            finish(m)
-            late_codes = held.tile([P, P], U32, name=f"carried{m}", align_bytes=64)
-            sums.append(value_product(2 + m, late_codes[:]))
-        for m in range(2, 4):
+        for m in range(2, VALUE_TILES):
+            finish(m - 2)
+            picked_vals = shared.tile(
+                [P, I], BF16, name=f"picked_vals{m}", align_bytes=64, offset=half_bytes + P * 4 + (m - 2) * I * 2
+            )
+            val_codes = held.tile([P, P], U32, name=f"carried{m - 2}", align_bytes=64)
+            values_mx.append(quantise_values(m, picked_vals, val_codes))
+            multiply(m, slice(0, J))
+        for m in range(2, VALUE_TILES):
             carry(m)
-            finish(m)
+            finish(m, HALF if m == VALUE_TILES - 1 else J)

from contextlib import ExitStack

import concourse.mybir as mybir
from concourse.masks import make_identity

D, T, I, J, U, E = 512, 2048, 512, 512, 1024, 512
FLOPS = 2 * D * I * U + 2 * I * E * J

F32 = mybir.dt.float32
BF16 = mybir.dt.bfloat16
I32 = mybir.dt.int32
U32 = mybir.dt.uint32
U16 = mybir.dt.uint16
U8 = mybir.dt.uint8
FP8X4 = mybir.dt.float8_e4m3fn_x4
ALU = mybir.AluOpType
COPY = mybir.ActivationFunctionType.Copy

P = 128
PACK = 4
BANK = 512
LIST_GROUP = 16
QUADRANT = 32
LINE = 4
PIECE = 256
SHARED_PIECE = 1
HALF = J // 2
VALUE_TILES = E // P


def by_lines(interleaved, planes):
    return (
        interleaved.rearrange("p (c i) t -> p c t i", i=LINE),
        [plane.rearrange("p t (c i) -> p c t i", i=LINE) for plane in planes],
    )


def tile_attend_tab_middleof3_changes_kernel(
    tc, keys_words, keys_scales, notes, rowf, vals, mem, offs, offs2, offs3, offs4, out
):
    nc = tc.nc
    with ExitStack() as ctx:
        held = ctx.enter_context(tc.tile_pool(name="held", bufs=1))
        work = ctx.enter_context(tc.tile_pool(name="work", bufs=PACK))
        shared = ctx.enter_context(tc.tile_pool(name="shared", bufs=1))
        psum = ctx.enter_context(tc.psum_pool(name="psum", bufs=1))

        def load_list(name, source):
            entries = held.tile([P, J // LIST_GROUP], U16, name=name)
            nc.sync.dma_start(entries[:], source)
            return entries

        def load_notes(n):
            raw = held.tile([P, PACK, PIECE], F32, name=f"notes_raw{n}")
            columns = notes[:, n * PIECE : (n + 1) * PIECE]
            nc.sync.dma_start(raw[:], columns.rearrange("(p t) u -> p t u", t=PACK))
            return raw

        token_list = load_list("token_list", offs)
        row_factor = held.tile([P, PACK], F32, name="row_factor")
        nc.sync.dma_start(row_factor[:], rowf.rearrange("(p t) o -> p (t o)", t=PACK))
        notes_raw = [load_notes(0)]

        key_scales = held.tile([P, T], U8, name="key_scales")
        nc.vector.memset(key_scales[:].bitcast(I32), 0)
        for q in range(P // QUADRANT):
            nc.sync.dma_start(
                key_scales[QUADRANT * q : QUADRANT * q + 4, :].bitcast(I32),
                keys_scales[0, 4 * q : 4 * q + 4, :].bitcast(I32),
            )
        key_words = held.tile([P, T], I32, name="key_words")
        nc.sync.dma_start(key_words[:], keys_words[0].rearrange("p n t -> p (n t)").bitcast(I32))
        notes_raw.extend(load_notes(n) for n in range(1, U // PIECE))

        first_list = load_list("first_list", offs2)
        second_list = load_list("second_list", offs3)
        third_list = load_list("third_list", offs4)

        vals_pool = []
        for m in range(VALUE_TILES):
            pool_rows = held.tile([P, T], F32, name=f"vals_pool{m}")
            nc.sync.dma_start(pool_rows[:], vals[m * P : (m + 1) * P, :])
            vals_pool.append(pool_rows)

        memory = held.tile([P, J], F32, name="memory")
        nc.sync.dma_start(memory[:], mem[0].partition_broadcast(P))

        identity = held.tile([P, P], F32, name="identity")
        make_identity(nc, identity[:])

        carried = []
        for m in range(VALUE_TILES):
            shifted = held.tile([P, J], F32, name=f"carried{m}", align_bytes=64)
            nc.vector.memset(shifted[:, 0:1], 0.0)
            carried.append(shifted)

        factor_rows = held.tile([P, PACK, J], F32, name="factor_rows")
        nc.scalar.copy(factor_rows[:], row_factor[:].unsqueeze(2).to_broadcast([P, PACK, J]))

        picked_scales = held.tile([P, I], U8, name="picked_scales", align_bytes=64)
        nc.vector.tensor_copy(
            picked_scales[:].rearrange("p (t s) -> p s t", t=PACK),
            key_scales[:].indirect(token_list[:]),
        )
        picked_words = held.tile([P, I], U32, name="picked_words", align_bytes=64)
        nc.vector.tensor_copy(
            picked_words[:].rearrange("p (t s) -> p s t", t=PACK),
            key_words[:].bitcast(U32).indirect(token_list[:]),
        )

        def round_notes(n):
            grouped = held.tile([P, PIECE, PACK], BF16, name=f"notes_grouped{n}", align_bytes=64)
            split = PIECE // 2 if n == SHARED_PIECE else PIECE
            target, (source,) = by_lines(grouped[:, :split, :], [notes_raw[n][:, :, :split]])
            nc.vector.tensor_copy(target, source)
            if split < PIECE:
                target, (source,) = by_lines(grouped[:, split:, :], [notes_raw[n][:, :, split:]])
                nc.scalar.copy(target, source)
            return grouped

        def quantise_notes(n):
            codes = held.tile([P, PIECE], U32, name=f"note_codes{n}", align_bytes=64)
            scales = held.tile([P, PIECE], U8, name=f"note_scales{n}", align_bytes=64)
            nc.vector.quantize_mx(
                out=codes[:].bitcast(FP8X4),
                scales=scales[:],
                in_=notes_grouped[n][:].rearrange("p u t -> p (u t)"),
            )
            return codes, scales

        notes_grouped = [round_notes(0)]
        notes_mx = []
        for n in range(U // PIECE):
            if n + 1 < U // PIECE:
                notes_grouped.append(round_notes(n + 1))
            notes_mx.append(quantise_notes(n))

        table = [held.tile([P, U], F32, name=f"table{t}") for t in range(PACK)]
        banks = [psum.tile([P, BANK], F32, name=f"bank{b}") for b in range(2 * PACK)]
        for b in range(2 * PACK):
            half, t = divmod(b, PACK)
            for column in range(0, BANK, PIECE):
                codes, scales = notes_mx[(half * BANK + column) // PIECE]
                nc.tensor.matmul_mx(
                    out=banks[b][:, column : column + PIECE],
                    lhsT=picked_words[:, t * P : (t + 1) * P].bitcast(FP8X4),
                    lhsT_scale=picked_scales[:, t * P : (t + 1) * P],
                    rhs=codes[:].bitcast(FP8X4),
                    rhs_scale=scales[:],
                    start=True,
                    stop=True,
                )
        for t in range(PACK):
            nc.scalar.copy(table[t][:, :BANK], banks[t][:])

        lower = held.tile([P, PACK, J], F32, name="lower")
        capped = held.tile([P, PACK, J], F32, name="capped")

        def look_up_second(t):
            second = work.tile([P, J], F32, name="second")
            nc.vector.tensor_tensor(second[:], table[t][:].indirect(second_list[:]), factor_rows[:, t, :], ALU.mult)
            return second

        nc.vector.tensor_copy(table[0][:, BANK:], banks[PACK][:])
        seconds = [look_up_second(0)]
        for t in range(PACK):
            if t + 1 < PACK:
                nc.scalar.copy(table[t + 1][:, BANK:], banks[PACK + t + 1][:])
                seconds.append(look_up_second(t + 1))
            first = work.tile([P, J], F32, name="first")
            third = work.tile([P, J], F32, name="third")
            upper = work.tile([P, J], F32, name="upper")
            nc.scalar.activation(first[:], table[t][:].indirect(first_list[:]), COPY)
            nc.scalar.activation(third[:], table[t][:].indirect(third_list[:]), COPY)
            factor = row_factor[:, t : t + 1]
            nc.vector.scalar_tensor_tensor(upper[:], first[:], factor, seconds[t][:], ALU.mult, ALU.max)
            nc.vector.scalar_tensor_tensor(lower[:, t, :], first[:], factor, seconds[t][:], ALU.mult, ALU.min)
            nc.vector.scalar_tensor_tensor(capped[:, t, :], third[:], factor, upper[:], ALU.mult, ALU.min)

        half_bytes = HALF * PACK * 2
        middle = []
        for h in range(2):
            rounded = shared.tile([P, HALF, PACK], BF16, name=f"middle{h}", align_bytes=64, offset=h * half_bytes)
            columns = slice(h * HALF, (h + 1) * HALF)
            target, (low, cap) = by_lines(rounded[:], [lower[:, :, columns], capped[:, :, columns]])
            nc.vector.tensor_tensor(target, low, cap, ALU.max)
            middle.append(rounded)
        middle_codes = held.tile([P, J], U32, name="middle_codes", align_bytes=64)
        middle_scales = held.tile([P, J], U8, name="middle_scales", align_bytes=64)

        def quantise_middle(h):
            columns = slice(h * HALF, (h + 1) * HALF)
            nc.vector.quantize_mx(
                out=middle_codes[:, columns].bitcast(FP8X4),
                scales=middle_scales[:, columns],
                in_=middle[h][:].rearrange("p j t -> p (j t)"),
            )

        def quantise_values(m, picked_vals, val_codes):
            nc.scalar.activation(picked_vals[:], vals_pool[m][:].indirect(token_list[:]), COPY)
            pairs = picked_vals[:].bitcast(F32)
            turned = psum.tile([P, 2, P], F32, name=f"bank{m}")
            for u in range(2):
                nc.tensor.transpose(turned[:, u, :], pairs[:, u : I // 2 : 2], identity[:])
            val_pairs = held.tile([P, P, 2], F32, name=f"val_pairs{m}", align_bytes=64)
            nc.scalar.copy(val_pairs[:], turned[:].rearrange("p u e -> p e u"))
            val_scales = held.tile([P, P], U8, name=f"val_scales{m}", align_bytes=64)
            nc.vector.quantize_mx(
                out=val_codes[:].bitcast(FP8X4),
                scales=val_scales[:],
                in_=val_pairs[:].rearrange("p e u -> p (e u)").bitcast(BF16),
            )
            return val_codes, val_scales

        def multiply(m, columns):
            val_codes, val_scales = values_mx[m]
            nc.tensor.matmul_mx(
                out=sums[m][:, columns],
                lhsT=val_codes[:].bitcast(FP8X4),
                lhsT_scale=val_scales[:],
                rhs=middle_codes[:, columns].bitcast(FP8X4),
                rhs_scale=middle_scales[:, columns],
                start=True,
                stop=True,
            )

        def carry(m):
            nc.vector.tensor_tensor(carried[m][:, 1:], sums[m][:, : J - 1], memory[:, 1:], ALU.mult)

        def finish(m, width=J):
            result = held.tile([P, J], F32, name=f"result{m}")
            for column in range(0, J, width):
                columns = slice(column, column + width)
                nc.vector.tensor_tensor(result[:, columns], sums[m][:, columns], carried[m][:, columns], ALU.subtract)
                nc.sync.dma_start(out[m * P : (m + 1) * P, columns], result[:, columns])

        sums = [psum.tile([P, J], F32, name=f"bank{PACK + m}") for m in range(VALUE_TILES)]
        values_mx = []
        for m in range(2):
            quantise_middle(m)
            picked_vals = held.tile([P, I], BF16, name=f"table{2 + m}")
            val_codes = shared.tile([P, P], U32, name=f"val_codes{m}", align_bytes=64, offset=m * half_bytes)
            values_mx.append(quantise_values(m, picked_vals, val_codes))
            multiply(0, slice(m * HALF, (m + 1) * HALF))
        multiply(1, slice(0, J))
        carry(0)
        carry(1)
        for m in range(2, VALUE_TILES):
            finish(m - 2)
            picked_vals = shared.tile(
                [P, I], BF16, name=f"picked_vals{m}", align_bytes=64, offset=half_bytes + P * 4 + (m - 2) * I * 2
            )
            val_codes = held.tile([P, P], U32, name=f"carried{m - 2}", align_bytes=64)
            values_mx.append(quantise_values(m, picked_vals, val_codes))
            multiply(m, slice(0, J))
        for m in range(2, VALUE_TILES):
            carry(m)
            finish(m, HALF if m == VALUE_TILES - 1 else J)
